import numpy as np
import ml_dtypes


def mxq(x, axis, fmt="e4m3"):
    dtype, down = {"e4m3": (ml_dtypes.float8_e4m3fn, 7), "e5m2": (ml_dtypes.float8_e5m2, 14)}[fmt]
    v = np.moveaxis(np.asarray(x, np.float32).astype(ml_dtypes.bfloat16).astype(np.float64), axis, -1)
    blocks = v.reshape(v.shape[:-1] + (-1, 32))
    amax = np.abs(blocks).max(-1, keepdims=True)
    byte = np.maximum(np.where(amax > 0, np.frexp(amax)[1] - 1 + 127, 0) - down, 1)
    scale = np.exp2(byte - 127.0)
    codes = (blocks / scale).astype(np.float32).astype(dtype).astype(np.float64)
    return np.moveaxis((codes * scale).reshape(v.shape), -1, axis)


WIDE = False


def mx_kscale(k):
    if not WIDE:
        return np.ones(k)
    levels = np.array([10, -10, 5, -5, 0])
    if k % 512:
        return np.exp2(np.random.permutation(np.resize(levels, k // 32))).repeat(32)
    a = np.empty((k // 512, 16))
    for p in range(k // 512):
        a[p, :8] = np.random.permutation(np.resize(levels, 8))
        for g in range(8):
            far = levels[np.abs(levels - a[p, g]) >= 10]
            a[p, g + 8] = far[np.random.randint(len(far))]
    return np.exp2(a.ravel()).repeat(32)


def f64(x):
    return np.asarray(x).astype(np.float64)


def striped(idx):
    return np.tile(idx.reshape(-1, 16).T, (8, 1)).astype(np.uint16)


def unstriped(offs):
    return offs[:16].T.reshape(-1).astype(np.int64)


def pack_weight(w):
    k, n = w.shape
    w = f64(np.asarray(w, np.float32).astype(ml_dtypes.bfloat16)).reshape(k // 32, 32, n)
    amax = np.abs(w).max(1)
    byte = np.clip(np.where(amax > 0, np.frexp(amax)[1] - 1 + 127 - 7, 1), 1, 254)
    scaled = (w * np.exp2(127.0 - byte)[:, None, :]).reshape(k, n).astype(np.float32)
    words = np.ascontiguousarray(scaled.reshape(k // 512, 128, 4, n).transpose(0, 1, 3, 2)).astype(ml_dtypes.float8_e4m3fn).view(np.uint8)
    return words, np.ascontiguousarray(byte.astype(np.uint8).reshape(k // 512, 16, n))


def unpack_weight(words, scales):
    g, p, n, _ = words.shape
    vals = np.ascontiguousarray(words).view(ml_dtypes.float8_e4m3fn).astype(np.float64) * np.repeat(np.exp2(scales.astype(np.float64) - 127.0), 8, axis=1)[..., None]
    return vals.transpose(0, 1, 3, 2).reshape(g * 512, n)


K, T, E, C, N = 1536, 1536, 4, 128, 384


def by_expert(wq, xq):
    return np.concatenate([wq[e].T @ xq[:, e * C:(e + 1) * C] for e in range(E)], axis=1)


def setup_inputs():
    n = np.random.standard_normal
    s = mx_kscale(K)[:, None]
    packed = [pack_weight(m) for m in n((E, K, N)) / np.sqrt(K) / s[None]]
    return {
        "xT": (n((K, T)) * s).astype(np.float32),
        "w_words": np.stack([m[0] for m in packed]),
        "w_scales": np.stack([m[1] for m in packed]),
        "gate": np.tile(np.random.uniform(0.2, 1.0, E * C), (N, 1)).astype(np.float32),
        "offs": striped(np.random.permutation(T)[:E * C]),
    }


def reference(xT, w_words, w_scales, gate, offs):
    idx = unstriped(offs)
    xq = mxq(f64(xT)[:, idx], 0, "e4m3")
    w = np.stack([unpack_weight(w_words[e], w_scales[e]) for e in range(E)])
    y = by_expert(w, xq)
    out = np.zeros((N, T))
    out[:, idx] = f64(gate) * y
    return out

@@ -1,0 +1,154 @@
+from contextlib import ExitStack
+
+import concourse.mybir as mybir
+
+K, T, E, C, N = 1536, 1536, 4, 128, 384
+SLOTS = E * C
+P = 128
+PASS = 512
+PASSES = K // PASS
+BLOCKS = N // P
+
+FLOPS = 2 * K * N * SLOTS
+BYTES = 4 * K * T + E * K * N + E * K * N // 32 + 4 * SLOTS + 2 * P * SLOTS // 16 + 4 * N * T
+
+F32 = mybir.dt.float32
+BF16 = mybir.dt.bfloat16
+U32 = mybir.dt.uint32
+I32 = mybir.dt.int32
+U16 = mybir.dt.uint16
+U8 = mybir.dt.uint8
+FP8X4 = mybir.dt.float8_e4m3fn_x4
+MULT = mybir.AluOpType.mult
+
+CHUNKS = [(0, 576, 768), (768, 1344, 1536)]
+LAST_CHUNKS = [(0, 576, 768), (768, 896, 1280), (1280, 1376, 1536)]
+
+
+def tile_routed_moe_kernel(tc, xT, w_words, w_scales, gate, offs, out):
+    nc = tc.nc
+    x_view = xT.rearrange("(g p u v) n -> g u p v n", p=P, u=2, v=2)
+    w_view = w_words.rearrange("e a p n r -> p (e a) (n r)")
+    ws_view = w_scales.rearrange("e a q n -> (e a) q n")
+
+    with ExitStack() as ctx:
+        keep = ctx.enter_context(tc.tile_pool(name="keep", bufs=1))
+        psum = ctx.enter_context(tc.psum_pool(name="psum", bufs=1))
+
+        offsets = keep.tile([P, SLOTS // 16], U16, name="offsets")
+        gates = keep.tile([P, SLOTS], F32, name="gates")
+        w_scale = keep.tile([P, PASSES, N], U8, name="w_scale", align_bytes=64)
+        w_codes = [keep.tile([P, E * PASSES, P], U32, name=f"w_codes{m}", align_bytes=64) for m in range(BLOCKS)]
+        x_codes = keep.tile([P, PASSES, SLOTS], U32, name="x_codes", align_bytes=64)
+        x_scale = keep.tile([P, PASSES, SLOTS], U8, name="x_scale", align_bytes=64)
+        grouped = [keep.tile([P, SLOTS, 4], BF16, name=f"grouped{a}", align_bytes=64) for a in range(PASSES)]
+        sums = [keep.tile([P, SLOTS], F32, name=f"sums{m}") for m in range(BLOCKS)]
+        window = [keep.tile([P, T], F32, name=f"window{m}") for m in range(BLOCKS)]
+
+        nc.vector.memset(w_scale[:].rearrange("p c n -> p (c n)").bitcast(I32), 0)
+
+        def load_scales(i):
+            c, quad = divmod(i, 4)
+            nc.sync.dma_start(
+                out=w_scale[32 * quad : 32 * quad + 16, c, :].bitcast(I32),
+                in_=ws_view[4 * c : 4 * c + 4, 4 * quad : 4 * quad + 4, :].bitcast(I32),
+            )
+
+        raws, pairs = {}, {}
+        scale_dma = 0
+        for a in range(PASSES):
+            for u in range(2):
+                raw = keep.tile([P, 2, T], F32, name=f"raw{a}{u}")
+                raws[a, u] = raw
+                pairs[a, u] = keep.tile([P, T, 2], BF16, name=f"pairs{a}{u}", align_bytes=64)
+                for lo, mid, hi in LAST_CHUNKS if (a, u) == (PASSES - 1, 1) else CHUNKS:
+                    nc.sync.dma_start(out=raw[:, :, lo:hi], in_=x_view[a, u, :, :, lo:hi])
+                    if (a, u, lo) == (0, 0, 0):
+                        nc.sync.dma_start(offsets[:], offs)
+                    elif scale_dma < 12:
+                        load_scales(scale_dma)
+                        scale_dma += 1
+
+        def load_w(m, lo, hi):
+            nc.sync.dma_start(
+                out=w_codes[m][:, lo:hi, :].bitcast(I32),
+                in_=w_view[:, lo:hi, 4 * P * m : 4 * P * (m + 1)].bitcast(I32),
+            )
+
+        load_w(0, 0, 6)
+        nc.sync.dma_start(out=gates[:], in_=gate[0:P, :])
+        load_w(0, 6, 12)
+        load_w(1, 0, 12)
+        load_w(2, 0, 12)
+
+        for m in range(BLOCKS):
+            nc.vector.memset(window[m][:], 0.0)
+
+        def cast(a, u, lo, mid, hi):
+            src = raws[a, u][:].rearrange("p v n -> p n v")
+            nc.scalar.copy(out=pairs[a, u][:, lo:mid, :], in_=src[:, lo:mid, :])
+            nc.vector.tensor_copy(out=pairs[a, u][:, mid:hi, :], in_=src[:, mid:hi, :])
+
+        def gather(a, u, lo, hi):
+            dst = grouped[a][:].rearrange("p s v -> p (s v)").bitcast(U32).rearrange("p (s u) -> p s u", u=2)
+            src = pairs[a, u][:].rearrange("p t v -> p (t v)").bitcast(U32)
+            nc.vector.tensor_copy(out=dst[:, lo:hi, u], in_=src.indirect(offsets[:, lo // 16 : hi // 16]))
+
+        def quantize(a, lo, hi):
+            nc.vector.quantize_mx(
+                out=x_codes[:, a, lo:hi].bitcast(FP8X4),
+                scales=x_scale[:, a, lo:hi],
+                in_=grouped[a][:, lo:hi, :].rearrange("p s v -> p (s v)"),
+            )
+
+        def multiply(acc, m, e, a):
+            c, j = divmod(e * PASSES + a, 4)
+            slots = slice(e * C, (e + 1) * C)
+            nc.tensor.matmul_mx(
+                out=acc,
+                lhsT=w_codes[m][:, e * PASSES + a, :].bitcast(FP8X4),
+                lhsT_scale=w_scale[4 * j : P, c, m * P : (m + 1) * P],
+                rhs=x_codes[:, a, slots].bitcast(FP8X4),
+                rhs_scale=x_scale[:, a, slots],
+                start=(a == 0),
+                stop=(a == PASSES - 1),
+            )
+
+        def scatter(m, lo, hi):
+            nc.vector.tensor_tensor(
+                window[m][:].indirect(offsets[:, lo // 16 : hi // 16]), sums[m][:, lo:hi], gates[:, lo:hi], MULT
+            )
+
+        for a in range(PASSES):
+            last = a == PASSES - 1
+            for u in range(2):
+                for lo, mid, hi in LAST_CHUNKS if last and u == 1 else CHUNKS:
+                    cast(a, u, lo, mid, hi)
+                if not (last and u == 1):
+                    gather(a, u, 0, SLOTS)
+            if not last:
+                quantize(a, 0, SLOTS)
+
+        first = [psum.tile([P, C], F32, name=f"first{e}") for e in range(E)]
+        for a in range(PASSES - 1):
+            for e in range(E):
+                multiply(first[e][:], 0, e, a)
+        a = PASSES - 1
+        half = SLOTS // 2
+        for lo in (0, half):
+            gather(a, 1, lo, lo + half)
+            quantize(a, lo, lo + half)
+            for e in range(lo // C, (lo + half) // C):
+                multiply(first[e][:], 0, e, a)
+                nc.scalar.copy(out=sums[0][:, e * C : (e + 1) * C], in_=first[e][:])
+        for lo in (0, half):
+            scatter(0, lo, lo + half)
+        nc.sync.dma_start(out=out[0:P, :], in_=window[0][:])
+        for m in range(1, BLOCKS):
+            acc = psum.tile([P, SLOTS], F32, name=f"acc{m}")
+            for e in range(E):
+                for a in range(PASSES):
+                    multiply(acc[:, e * C : (e + 1) * C], m, e, a)
+            nc.scalar.copy(out=sums[m][:], in_=acc[:])
+            scatter(m, 0, SLOTS)
+            nc.sync.dma_start(out=out[m * P : (m + 1) * P, :], in_=window[m][:])

@@ -21,15 +21,21 @@ U8 = mybir.dt.uint8
 FP8X4 = mybir.dt.float8_e4m3fn_x4
 MULT = mybir.AluOpType.mult
 
-CHUNKS = [(0, 576, 768), (768, 1344, 1536)]
-LAST_CHUNKS = [(0, 576, 768), (768, 896, 1280), (1280, 1376, 1536)]
+CHUNKS = [
+    [(0, 320, T)],
+    [(0, 320, T)],
+    [(0, 704, T)],
+    [(0, 544, T)],
+    [(0, 544, T)],
+    [(0, 640, 640), (640, 960, 1152), (1152, 1216, T)],
+]
 
 
 def tile_routed_moe_kernel(tc, xT, w_words, w_scales, gate, offs, out):
     nc = tc.nc
     x_view = xT.rearrange("(g p u v) n -> g u p v n", p=P, u=2, v=2)
     w_view = w_words.rearrange("e a p n r -> p (e a) (n r)")
-    ws_view = w_scales.rearrange("e a q n -> (e a) q n")
+    ws_view = w_scales.rearrange("e a q n -> q (e a) n")
 
     with ExitStack() as ctx:
         keep = ctx.enter_context(tc.tile_pool(name="keep", bufs=1))
@@ -37,7 +43,7 @@ def tile_routed_moe_kernel(tc, xT, w_words, w_scales, gate, offs, out):
 
         offsets = keep.tile([P, SLOTS // 16], U16, name="offsets")
         gates = keep.tile([P, SLOTS], F32, name="gates")
-        w_scale = keep.tile([P, PASSES, N], U8, name="w_scale", align_bytes=64)
+        w_scale = keep.tile([P, E * PASSES, N], U8, name="w_scale", align_bytes=64)
         w_codes = [keep.tile([P, E * PASSES, P], U32, name=f"w_codes{m}", align_bytes=64) for m in range(BLOCKS)]
         x_codes = keep.tile([P, PASSES, SLOTS], U32, name="x_codes", align_bytes=64)
         x_scale = keep.tile([P, PASSES, SLOTS], U8, name="x_scale", align_bytes=64)
@@ -45,29 +51,24 @@ def tile_routed_moe_kernel(tc, xT, w_words, w_scales, gate, offs, out):
         sums = [keep.tile([P, SLOTS], F32, name=f"sums{m}") for m in range(BLOCKS)]
         window = [keep.tile([P, T], F32, name=f"window{m}") for m in range(BLOCKS)]
 
-        nc.vector.memset(w_scale[:].rearrange("p c n -> p (c n)").bitcast(I32), 0)
+        nc.gpsimd.memset(w_scale[:].rearrange("p c n -> p (c n)").bitcast(I32), 0)
 
-        def load_scales(i):
-            c, quad = divmod(i, 4)
+        def load_scales(quad):
             nc.sync.dma_start(
-                out=w_scale[32 * quad : 32 * quad + 16, c, :].bitcast(I32),
-                in_=ws_view[4 * c : 4 * c + 4, 4 * quad : 4 * quad + 4, :].bitcast(I32),
+                out=w_scale[32 * quad : 32 * quad + 4, :, :].bitcast(I32),
+                in_=ws_view[4 * quad : 4 * quad + 4, :, :].bitcast(I32),
             )
 
         raws, pairs = {}, {}
-        scale_dma = 0
         for a in range(PASSES):
             for u in range(2):
                 raw = keep.tile([P, 2, T], F32, name=f"raw{a}{u}")
                 raws[a, u] = raw
                 pairs[a, u] = keep.tile([P, T, 2], BF16, name=f"pairs{a}{u}", align_bytes=64)
-                for lo, mid, hi in LAST_CHUNKS if (a, u) == (PASSES - 1, 1) else CHUNKS:
+                for lo, mid, hi in CHUNKS[2 * a + u]:
                     nc.sync.dma_start(out=raw[:, :, lo:hi], in_=x_view[a, u, :, :, lo:hi])
                     if (a, u, lo) == (0, 0, 0):
                         nc.sync.dma_start(offsets[:], offs)
-                    elif scale_dma < 12:
-                        load_scales(scale_dma)
-                        scale_dma += 1
 
         def load_w(m, lo, hi):
             nc.sync.dma_start(
@@ -76,6 +77,8 @@ def tile_routed_moe_kernel(tc, xT, w_words, w_scales, gate, offs, out):
             )
 
         load_w(0, 0, 6)
+        for quad in range(4):
+            load_scales(quad)
         nc.sync.dma_start(out=gates[:], in_=gate[0:P, :])
         load_w(0, 6, 12)
         load_w(1, 0, 12)
@@ -87,7 +90,8 @@ def tile_routed_moe_kernel(tc, xT, w_words, w_scales, gate, offs, out):
         def cast(a, u, lo, mid, hi):
             src = raws[a, u][:].rearrange("p v n -> p n v")
             nc.scalar.copy(out=pairs[a, u][:, lo:mid, :], in_=src[:, lo:mid, :])
-            nc.vector.tensor_copy(out=pairs[a, u][:, mid:hi, :], in_=src[:, mid:hi, :])
+            if mid < hi:
+                nc.vector.tensor_copy(out=pairs[a, u][:, mid:hi, :], in_=src[:, mid:hi, :])
 
         def gather(a, u, lo, hi):
             dst = grouped[a][:].rearrange("p s v -> p (s v)").bitcast(U32).rearrange("p (s u) -> p s u", u=2)
@@ -102,12 +106,11 @@ def tile_routed_moe_kernel(tc, xT, w_words, w_scales, gate, offs, out):
             )
 
         def multiply(acc, m, e, a):
-            c, j = divmod(e * PASSES + a, 4)
             slots = slice(e * C, (e + 1) * C)
             nc.tensor.matmul_mx(
                 out=acc,
                 lhsT=w_codes[m][:, e * PASSES + a, :].bitcast(FP8X4),
-                lhsT_scale=w_scale[4 * j : P, c, m * P : (m + 1) * P],
+                lhsT_scale=w_scale[:, e * PASSES + a, m * P : (m + 1) * P],
                 rhs=x_codes[:, a, slots].bitcast(FP8X4),
                 rhs_scale=x_scale[:, a, slots],
                 start=(a == 0),
@@ -122,7 +125,7 @@ def tile_routed_moe_kernel(tc, xT, w_words, w_scales, gate, offs, out):
         for a in range(PASSES):
             last = a == PASSES - 1
             for u in range(2):
-                for lo, mid, hi in LAST_CHUNKS if last and u == 1 else CHUNKS:
+                for lo, mid, hi in CHUNKS[2 * a + u]:
                     cast(a, u, lo, mid, hi)
                 if not (last and u == 1):
                     gather(a, u, 0, SLOTS)

@@ -22,12 +22,12 @@ FP8X4 = mybir.dt.float8_e4m3fn_x4
 MULT = mybir.AluOpType.mult
 
 CHUNKS = [
-    [(0, 320, T)],
-    [(0, 320, T)],
-    [(0, 704, T)],
-    [(0, 544, T)],
-    [(0, 544, T)],
-    [(0, 640, 640), (640, 960, 1152), (1152, 1216, T)],
+    [(0, 608, T)],
+    [(0, 672, T)],
+    [(0, 928, T)],
+    [(0, 768, 768), (768, 1184, T)],
+    [(0, 768, 768), (768, 1200, T)],
+    [(0, 640, 640), (640, 832, 1152), (1152, 1216, T)],
 ]
 
 
@@ -88,10 +88,12 @@ def tile_routed_moe_kernel(tc, xT, w_words, w_scales, gate, offs, out):
             nc.vector.memset(window[m][:], 0.0)
 
         def cast(a, u, lo, mid, hi):
-            src = raws[a, u][:].rearrange("p v n -> p n v")
-            nc.scalar.copy(out=pairs[a, u][:, lo:mid, :], in_=src[:, lo:mid, :])
+            src = raws[a, u][:].rearrange("p v (c i) -> p c v i", i=4)
+            dst = pairs[a, u][:].rearrange("p (c i) v -> p c v i", i=4)
+            lo, mid, hi = lo // 4, mid // 4, hi // 4
+            nc.scalar.copy(out=dst[:, lo:mid], in_=src[:, lo:mid])
             if mid < hi:
-                nc.vector.tensor_copy(out=pairs[a, u][:, mid:hi, :], in_=src[:, mid:hi, :])
+                nc.vector.tensor_copy(out=dst[:, mid:hi], in_=src[:, mid:hi])
 
         def gather(a, u, lo, hi):
             dst = grouped[a][:].rearrange("p s v -> p (s v)").bitcast(U32).rearrange("p (s u) -> p s u", u=2)
@@ -133,16 +135,16 @@ def tile_routed_moe_kernel(tc, xT, w_words, w_scales, gate, offs, out):
                 quantize(a, 0, SLOTS)
 
         first = [psum.tile([P, C], F32, name=f"first{e}") for e in range(E)]
-        for a in range(PASSES - 1):
-            for e in range(E):
-                multiply(first[e][:], 0, e, a)
-        a = PASSES - 1
         half = SLOTS // 2
         for lo in (0, half):
-            gather(a, 1, lo, lo + half)
-            quantize(a, lo, lo + half)
-            for e in range(lo // C, (lo + half) // C):
-                multiply(first[e][:], 0, e, a)
+            experts = range(lo // C, (lo + half) // C)
+            for e in experts:
+                for a in range(PASSES - 1):
+                    multiply(first[e][:], 0, e, a)
+            gather(PASSES - 1, 1, lo, lo + half)
+            quantize(PASSES - 1, lo, lo + half)
+            for e in experts:
+                multiply(first[e][:], 0, e, PASSES - 1)
                 nc.scalar.copy(out=sums[0][:, e * C : (e + 1) * C], in_=first[e][:])
         for lo in (0, half):
             scatter(0, lo, lo + half)

@@ -22,12 +22,12 @@ FP8X4 = mybir.dt.float8_e4m3fn_x4
 MULT = mybir.AluOpType.mult
 
 CHUNKS = [
+    [(0, 544, T)],
     [(0, 608, T)],
-    [(0, 672, T)],
-    [(0, 928, T)],
-    [(0, 768, 768), (768, 1184, T)],
-    [(0, 768, 768), (768, 1200, T)],
-    [(0, 640, 640), (640, 832, 1152), (1152, 1216, T)],
+    [(0, 800, T)],
+    [(0, 704, T)],
+    [(0, 512, 768), (768, 1152, T)],
+    [(0, 640, 640), (640, 896, 1280), (1280, 1360, T)],
 ]
 
 
@@ -53,11 +53,12 @@ def tile_routed_moe_kernel(tc, xT, w_words, w_scales, gate, offs, out):
 
         nc.gpsimd.memset(w_scale[:].rearrange("p c n -> p (c n)").bitcast(I32), 0)
 
-        def load_scales(quad):
-            nc.sync.dma_start(
-                out=w_scale[32 * quad : 32 * quad + 4, :, :].bitcast(I32),
-                in_=ws_view[4 * quad : 4 * quad + 4, :, :].bitcast(I32),
-            )
+        def load_scales(lo, hi):
+            for quad in range(4):
+                nc.sync.dma_start(
+                    out=w_scale[32 * quad : 32 * quad + 4, lo:hi, :].bitcast(I32),
+                    in_=ws_view[4 * quad : 4 * quad + 4, lo:hi, :].bitcast(I32),
+                )
 
         raws, pairs = {}, {}
         for a in range(PASSES):
@@ -76,11 +77,11 @@ def tile_routed_moe_kernel(tc, xT, w_words, w_scales, gate, offs, out):
                 in_=w_view[:, lo:hi, 4 * P * m : 4 * P * (m + 1)].bitcast(I32),
             )
 
-        load_w(0, 0, 6)
-        for quad in range(4):
-            load_scales(quad)
-        nc.sync.dma_start(out=gates[:], in_=gate[0:P, :])
-        load_w(0, 6, 12)
+        half = SLOTS // 2
+        for h in range(2):
+            load_w(0, 6 * h, 6 * h + 6)
+            load_scales(6 * h, 6 * h + 6)
+            nc.sync.dma_start(out=gates[:, h * half : (h + 1) * half], in_=gate[0:P, h * half : (h + 1) * half])
         load_w(1, 0, 12)
         load_w(2, 0, 12)
 
@@ -88,12 +89,10 @@ def tile_routed_moe_kernel(tc, xT, w_words, w_scales, gate, offs, out):
             nc.vector.memset(window[m][:], 0.0)
 
         def cast(a, u, lo, mid, hi):
-            src = raws[a, u][:].rearrange("p v (c i) -> p c v i", i=4)
-            dst = pairs[a, u][:].rearrange("p (c i) v -> p c v i", i=4)
-            lo, mid, hi = lo // 4, mid // 4, hi // 4
-            nc.scalar.copy(out=dst[:, lo:mid], in_=src[:, lo:mid])
+            src = raws[a, u][:].rearrange("p v n -> p n v")
+            nc.scalar.copy(out=pairs[a, u][:, lo:mid, :], in_=src[:, lo:mid, :])
             if mid < hi:
-                nc.vector.tensor_copy(out=dst[:, mid:hi], in_=src[:, mid:hi])
+                nc.vector.tensor_copy(out=pairs[a, u][:, mid:hi, :], in_=src[:, mid:hi, :])
 
         def gather(a, u, lo, hi):
             dst = grouped[a][:].rearrange("p s v -> p (s v)").bitcast(U32).rearrange("p (s u) -> p s u", u=2)
@@ -135,7 +134,6 @@ def tile_routed_moe_kernel(tc, xT, w_words, w_scales, gate, offs, out):
                 quantize(a, 0, SLOTS)
 
         first = [psum.tile([P, C], F32, name=f"first{e}") for e in range(E)]
-        half = SLOTS // 2
         for lo in (0, half):
             experts = range(lo // C, (lo + half) // C)
             for e in experts:

from contextlib import ExitStack

import concourse.mybir as mybir

K, T, E, C, N = 1536, 1536, 4, 128, 384
SLOTS = E * C
P = 128
PASS = 512
PASSES = K // PASS
BLOCKS = N // P

FLOPS = 2 * K * N * SLOTS
BYTES = 4 * K * T + E * K * N + E * K * N // 32 + 4 * SLOTS + 2 * P * SLOTS // 16 + 4 * N * T

F32 = mybir.dt.float32
BF16 = mybir.dt.bfloat16
U32 = mybir.dt.uint32
I32 = mybir.dt.int32
U16 = mybir.dt.uint16
U8 = mybir.dt.uint8
FP8X4 = mybir.dt.float8_e4m3fn_x4
MULT = mybir.AluOpType.mult

CHUNKS = [
    [(0, 544, T)],
    [(0, 608, T)],
    [(0, 800, T)],
    [(0, 704, T)],
    [(0, 512, 768), (768, 1152, T)],
    [(0, 640, 640), (640, 896, 1280), (1280, 1360, T)],
]


def tile_routed_moe_kernel(tc, xT, w_words, w_scales, gate, offs, out):
    nc = tc.nc
    x_view = xT.rearrange("(g p u v) n -> g u p v n", p=P, u=2, v=2)
    w_view = w_words.rearrange("e a p n r -> p (e a) (n r)")
    ws_view = w_scales.rearrange("e a q n -> q (e a) n")

    with ExitStack() as ctx:
        keep = ctx.enter_context(tc.tile_pool(name="keep", bufs=1))
        psum = ctx.enter_context(tc.psum_pool(name="psum", bufs=1))

        offsets = keep.tile([P, SLOTS // 16], U16, name="offsets")
        gates = keep.tile([P, SLOTS], F32, name="gates")
        w_scale = keep.tile([P, E * PASSES, N], U8, name="w_scale", align_bytes=64)
        w_codes = [keep.tile([P, E * PASSES, P], U32, name=f"w_codes{m}", align_bytes=64) for m in range(BLOCKS)]
        x_codes = keep.tile([P, PASSES, SLOTS], U32, name="x_codes", align_bytes=64)
        x_scale = keep.tile([P, PASSES, SLOTS], U8, name="x_scale", align_bytes=64)
        grouped = [keep.tile([P, SLOTS, 4], BF16, name=f"grouped{a}", align_bytes=64) for a in range(PASSES)]
        sums = [keep.tile([P, SLOTS], F32, name=f"sums{m}") for m in range(BLOCKS)]
        window = [keep.tile([P, T], F32, name=f"window{m}") for m in range(BLOCKS)]

        nc.gpsimd.memset(w_scale[:].rearrange("p c n -> p (c n)").bitcast(I32), 0)

        def load_scales(lo, hi):
            for quad in range(4):
                nc.sync.dma_start(
                    out=w_scale[32 * quad : 32 * quad + 4, lo:hi, :].bitcast(I32),
                    in_=ws_view[4 * quad : 4 * quad + 4, lo:hi, :].bitcast(I32),
                )

        raws, pairs = {}, {}
        for a in range(PASSES):
            for u in range(2):
                raw = keep.tile([P, 2, T], F32, name=f"raw{a}{u}")
                raws[a, u] = raw
                pairs[a, u] = keep.tile([P, T, 2], BF16, name=f"pairs{a}{u}", align_bytes=64)
                for lo, mid, hi in CHUNKS[2 * a + u]:
                    nc.sync.dma_start(out=raw[:, :, lo:hi], in_=x_view[a, u, :, :, lo:hi])
                    if (a, u, lo) == (0, 0, 0):
                        nc.sync.dma_start(offsets[:], offs)

        def load_w(m, lo, hi):
            nc.sync.dma_start(
                out=w_codes[m][:, lo:hi, :].bitcast(I32),
                in_=w_view[:, lo:hi, 4 * P * m : 4 * P * (m + 1)].bitcast(I32),
            )

        half = SLOTS // 2
        for h in range(2):
            load_w(0, 6 * h, 6 * h + 6)
            load_scales(6 * h, 6 * h + 6)
            nc.sync.dma_start(out=gates[:, h * half : (h + 1) * half], in_=gate[0:P, h * half : (h + 1) * half])
        load_w(1, 0, 12)
        load_w(2, 0, 12)

        for m in range(BLOCKS):
            nc.vector.memset(window[m][:], 0.0)

        def cast(a, u, lo, mid, hi):
            src = raws[a, u][:].rearrange("p v n -> p n v")
            nc.scalar.copy(out=pairs[a, u][:, lo:mid, :], in_=src[:, lo:mid, :])
            if mid < hi:
                nc.vector.tensor_copy(out=pairs[a, u][:, mid:hi, :], in_=src[:, mid:hi, :])

        def gather(a, u, lo, hi):
            dst = grouped[a][:].rearrange("p s v -> p (s v)").bitcast(U32).rearrange("p (s u) -> p s u", u=2)
            src = pairs[a, u][:].rearrange("p t v -> p (t v)").bitcast(U32)
            nc.vector.tensor_copy(out=dst[:, lo:hi, u], in_=src.indirect(offsets[:, lo // 16 : hi // 16]))

        def quantize(a, lo, hi):
            nc.vector.quantize_mx(
                out=x_codes[:, a, lo:hi].bitcast(FP8X4),
                scales=x_scale[:, a, lo:hi],
                in_=grouped[a][:, lo:hi, :].rearrange("p s v -> p (s v)"),
            )

        def multiply(acc, m, e, a):
            slots = slice(e * C, (e + 1) * C)
            nc.tensor.matmul_mx(
                out=acc,
                lhsT=w_codes[m][:, e * PASSES + a, :].bitcast(FP8X4),
                lhsT_scale=w_scale[:, e * PASSES + a, m * P : (m + 1) * P],
                rhs=x_codes[:, a, slots].bitcast(FP8X4),
                rhs_scale=x_scale[:, a, slots],
                start=(a == 0),
                stop=(a == PASSES - 1),
            )

        def scatter(m, lo, hi):
            nc.vector.tensor_tensor(
                window[m][:].indirect(offsets[:, lo // 16 : hi // 16]), sums[m][:, lo:hi], gates[:, lo:hi], MULT
            )

        for a in range(PASSES):
            last = a == PASSES - 1
            for u in range(2):
                for lo, mid, hi in CHUNKS[2 * a + u]:
                    cast(a, u, lo, mid, hi)
                if not (last and u == 1):
                    gather(a, u, 0, SLOTS)
            if not last:
                quantize(a, 0, SLOTS)

        first = [psum.tile([P, C], F32, name=f"first{e}") for e in range(E)]
        for lo in (0, half):
            experts = range(lo // C, (lo + half) // C)
            for e in experts:
                for a in range(PASSES - 1):
                    multiply(first[e][:], 0, e, a)
            gather(PASSES - 1, 1, lo, lo + half)
            quantize(PASSES - 1, lo, lo + half)
            for e in experts:
                multiply(first[e][:], 0, e, PASSES - 1)
                nc.scalar.copy(out=sums[0][:, e * C : (e + 1) * C], in_=first[e][:])
        for lo in (0, half):
            scatter(0, lo, lo + half)
        nc.sync.dma_start(out=out[0:P, :], in_=window[0][:])
        for m in range(1, BLOCKS):
            acc = psum.tile([P, SLOTS], F32, name=f"acc{m}")
            for e in range(E):
                for a in range(PASSES):
                    multiply(acc[:, e * C : (e + 1) * C], m, e, a)
            nc.scalar.copy(out=sums[m][:], in_=acc[:])
            scatter(m, 0, SLOTS)
            nc.sync.dma_start(out=out[m * P : (m + 1) * P, :], in_=window[m][:])
